import numpy as np, ml_dtypes
CORES = [16,32,48,64,80]
N = 5
V, K, ROUNDS = 4096, 4, 3
def entries(a): return a.T.reshape(-1)
def pack(v, P): return np.ascontiguousarray(np.asarray(v, np.int32).reshape(-1, P).T)
def lists(rng, how):
    T = V * K; me = np.arange(N)[:, None]
    I = rng.integers(0, N * V, (N, T))
    if how == "alike": I[:] = rng.integers(N * V)
    if how == "back": I = (V * me + np.arange(T)[None, :] // K - 1) % (N * V)
    if how == "edge": I = V * rng.integers(0, N, (N, T)) + np.where(rng.random((N, T)) < 0.5, 0, V - 1)
    if how == "hotrank": J = rng.integers(0, V, (N, T)); J[:, :V] = np.arange(V); I = V * int(rng.integers(N)) + rng.permuted(J, axis=1)
    if how == "line": I = np.minimum(V * me + np.arange(T)[None, :] // K + 1, N * V - 1)
    return {"nb": np.stack([pack(i, 16) for i in I])}
def setup_inputs(rng):
    return dict({"x": rng.standard_normal((N, 128, V), dtype=np.float32).astype(ml_dtypes.bfloat16)}, **lists(rng, "uniform"))
def setup_inputs_alike(rng):
    d = setup_inputs(rng); d.update(lists(rng, "alike"))
    for k in ("x",): d[k] = (d[k].astype(np.float32) * 1048576.0).astype(d[k].dtype)
    return d
def setup_inputs_back(rng):
    d = setup_inputs(rng); d.update(lists(rng, "back"))
    for k in ("x",): d[k] = (d[k].astype(np.float32) * (1 / 1024.0)).astype(d[k].dtype)
    return d
def setup_inputs_edge(rng):
    d = setup_inputs(rng); d.update(lists(rng, "edge"))
    return d
def setup_inputs_hotrank(rng):
    d = setup_inputs(rng); d.update(lists(rng, "hotrank"))
    return d
def setup_inputs_line(rng):
    d = setup_inputs(rng); d.update(lists(rng, "line"))
    return d
def check_inputs(x):
    bad = []
    if x["nb"].min() < 0 or x["nb"].max() >= N * V: bad.append("nb out of range")
    if np.abs(x["x"].astype(np.float32)).max() > 1e30: bad.append("x beyond -1e30 to 1e30")
    return bad
def reference(x, nb):
    A = np.concatenate(list(x), axis=1)
    NB = np.concatenate([entries(a) for a in nb]).reshape(N * V, K)
    for k in range(ROUNDS):
        B = A.copy()
        for j in range(K): B = np.maximum(B, A[:, NB[:, j]])
        A = B
    return {"y": np.stack([A[:, V * r:V * r + V] for r in range(N)])}

from concourse.bass import DstId, RemoteDMATransfer
from concourse.mybir import AluOpType, ActivationFunctionType

N, V, K = 5, 4096, 4
SIM_CORES = 96
NC = 32
NV = N * V
HB = 256
PE = HB * K
VSET = (1, 5)

SCRATCH = {
    "l32": ("sbuf", [128, 128], "int32"),
    "l16": ("sbuf", [128, 128], "uint16"),
    "lst": ("dram", [128, 128], "uint16"),
    "lin": ("dram", [128, 128], "uint16"),
    "offs": ("sbuf", [128, 128 * N], "uint16"),
    "xs": ("dram", [NC, 128, 128], "bfloat16"),
    "yl": ("dram", [NC, 128, 128], "bfloat16"),
    "d0": ("dram", [N, 128, 128], "bfloat16"),
    "d1": ("dram", [4, NV], "bfloat16"),
    "d2": ("dram", [4, NV], "bfloat16"),
    "d3": ("dram", [N, 128, 128], "bfloat16"),
    "w0": ("sbuf", [128, NV], "bfloat16"),
    "w1": ("sbuf", [128, NV], "bfloat16"),
    "gat": ("sbuf", [128, 10 * PE], "bfloat16"),
    "sx": ("sbuf", [128, 10 * PE], "bfloat16"),
    "pat": ("sbuf", [128, PE], "bfloat16"),
    "r0": ("sbuf", [128, 512 * N], "bfloat16"),
    "r1": ("sbuf", [128, 512 * N], "bfloat16"),
    "r2": ("sbuf", [128, 512 * N], "bfloat16"),
    "r3": ("sbuf", [128, 512 * N], "bfloat16"),
}
SEMAPHORES = (["loc", "nbl", "cv", "lstst", "yst", "lin", "la", "xf", "sv", "ss"]
              + ["xl%d" % i for i in range(N)] + ["xa%d" % i for i in range(N)] + ["ret%d" % i for i in range(N)]
              + ["rs%d" % i for i in range(N)] + ["rd%d_%d" % (k, c) for k in (1, 2) for c in range(3)] + ["fl1", "fl2"])


def plan(topo, cores):
    classes, first, n = [], [], 0
    for q in range(N):
        cnt = NC // N + (1 if q < NC % N else 0)
        mine = [c for c in range(SIM_CORES) if c != cores[q] and topo.chip(c) == topo.chip(cores[q])]
        classes.append(mine[:cnt])
        first.append(n)
        n += cnt
    return classes, first


def bits(m):
    return [b for b in range(m.bit_length()) if (m >> b) & 1]


def to_mask(bs):
    m = 0
    for b in bs:
        m |= 1 << b
    return m


def dst_id(topo, c):
    a = topo.addr(c)
    return DstId(rid=a[0], pnc=a[1])


def rank_program(g, core, T, topo):
    cores = [int(c) for c in T.cores]
    classes, first = plan(topo, cores)
    rank = T.rank_of(core)
    if rank is not None:
        rank_core(g, core, int(rank), T, topo, cores, classes, first)
        return
    for q in range(N):
        if core in classes[q]:
            compute_core(g, core, q, classes[q].index(core), T, topo, cores, classes, first)
            return


RET_E = 8


def rank_core(g, core, me, T, topo, cores, classes, first):
    order = [(me + 1) % N, me] + [(me + i) % N for i in range(2, N)]
    for i, q in enumerate(order):
        a, b = first[q], first[q] + len(classes[q])
        g.sync.dma_start(T.xs[a:b], T.x[4 * a:4 * b, :]).then_inc(T.sem["xl%d" % i], 16)
    for k in range(8):
        g.scalar.dma_start(T.l32[16 * k:16 * k + 16, :], T.nb[:, 128 * k:128 * k + 128]).then_inc(T.sem.nbl, 16)
    g.vector.wait_ge(T.sem.nbl, 128)
    g.vector.tensor_copy(T.l16[:], T.l32[:]).then_inc(T.sem.cv, 1)
    g.scalar.wait_ge(T.sem.cv, 1)
    g.scalar.dma_start(T.lst[:], T.l16[:]).then_inc(T.sem.lstst, 16)

    off = bits(topo.mask(core, classes[(me + 1) % N][0]))
    on = [b for b in bits(topo.mask(core, classes[me][0])) if b not in off]
    loc, nxt = 0, 0
    for i, q in enumerate(order):
        g.wait_ge(T.sem["xl%d" % i], 16)
        tr = []
        for k, c in enumerate(classes[q]):
            if q == me:
                e = on[k % len(on)]
            else:
                e = off[nxt % len(off)]
                nxt += 1
            tr.append(RemoteDMATransfer(dst_ids=[dst_id(topo, c)], dma_engine_mask=1 << e, remote_sem=T.sem["xa%d" % me],
                                        src=T.xs[first[q] + k], dst=T.d0[me]))
        g.remote_dma_fused(tr, local_sem=T.sem.loc)
        loc += len(tr)
        if i == 0:
            g.wait_ge(T.sem.lstst, 16)
            g.remote_dma_fused([RemoteDMATransfer(
                dst_ids=[dst_id(topo, classes[p][me]) for p in range(N)], dma_engine_mask=to_mask(off),
                remote_sem=T.sem.lin, srcs=[T.lst[:]], dsts=[T.lin[:] for p in range(N)])], local_sem=T.sem.loc)
            loc += len(off)
    g.wait_ge(T.sem.loc, loc)
    for s in range(N):
        q = (me - 1 - s) % N
        a, b = first[q], first[q] + len(classes[q])
        g.sync.wait_ge(T.sem["ret%d" % s], RET_E * (b - a))
        g.sync.dma_start(T.y[4 * a:4 * b, :], T.yl[a:b]).then_inc(T.sem.yst, 16)
    g.sync.wait_ge(T.sem.yst, 16 * N)


def compute_core(g, core, q, k, T, topo, cores, classes, first):
    j = first[q] + k
    W = [T.w0, T.w1]
    R = [T.r0, T.r1, T.r2, T.r3]
    nv = [0]
    ns = [0]

    def v(ins):
        ins.then_inc(T.sem.sv, 1)
        nv[0] += 1
        return nv[0]

    def sc(ins):
        ins.then_inc(T.sem.ss, 1)
        ns[0] += 1
        return ns[0]

    relay = k if k < N else None
    others = [c for c in classes[q] if c != core]
    full = to_mask(bits(topo.mask(core, others[0])))
    nfull = len(bits(full))
    off_in = len(bits(topo.mask(cores[q], classes[(q + 1) % N][0])))
    loc = 0
    if relay is not None:
        blk = slice(128 * relay, 128 * relay + 128)
        g.wait_ge(T.sem.lin, off_in)
        g.remote_dma_fused([RemoteDMATransfer(
            dst_ids=[dst_id(topo, c) for c in others], dma_engine_mask=full, remote_sem=T.sem.la,
            srcs=[T.lin[:]], dsts=[T.offs[:, blk] for c in others])], local_sem=T.sem.loc)
        loc += nfull
    la_total = nfull * (N - (1 if relay is not None else 0))

    arr = [(q - 1) % N, q] + [(q - i) % N for i in range(2, N)]
    z = v(g.vector.memset(T.gat[:, 0:V], 0.0))
    rz = v(g.vector.memset(T.r0[:], 0.0))
    wz = {}
    for p in arr[:1]:
        wz[p] = v(g.vector.memset(T.w0[:, V * p:V * p + V], 0.0))
    p1 = v(g.vector.memset(T.pat[:], 1e29))
    for p in arr[1:]:
        wz[p] = v(g.vector.memset(T.w0[:, V * p:V * p + V], 0.0))
    g.vector.wait_ge(T.sem.sv, p1)
    p2 = v(g.vector.memset(T.pat[:, 0:PE:K], -1e29))
    for p in range(3):
        v(g.vector.memset(T.w1[:, V * p:V * p + V], 0.0))
    g.vector.wait_ge(T.sem.sv, p2)
    v(g.vector.tensor_scalar(T.pat[:], T.pat[:], 1e7, None, AluOpType.mult))
    g.scalar.wait_ge(T.sem.sv, z)
    for p in range(3, N):
        sc(g.scalar.activation(T.w1[:, V * p:V * p + V], T.gat[:, 0:V], ActivationFunctionType.Copy))
    g.vector.wait_ge(T.sem.ss, ns[0])
    zs = ns[0]

    xf = 0
    for i, p in enumerate(arr):
        for h, eng in enumerate((g.sync, g.scalar)):
            eng.wait_ge(T.sem.sv, max(wz[p], rz))
            eng.wait_ge(T.sem["xa%d" % p], 1)
            for gg in range(4 * h, 4 * h + 4):
                eng.dma_start(T.w0[16 * gg:16 * gg + 4, V * p:V * p + V], T.d0[p]).then_inc(T.sem.xf, 16)
                xf += 16
            for r in range(2 * h, 2 * h + 2):
                eng.dma_start(T.r0[r:128:16, 512 * p:512 * p + 512], T.d0[p, 32 * r:32 * r + 32, :]).then_inc(T.sem.xf, 16)
                xf += 16
        if i == 0 and relay is not None:
            g.sync.wait_ge(T.sem.lin, off_in)
            g.sync.dma_start(T.offs[:, blk], T.lin[:]).then_inc(T.sem.xf, 16)
            xf += 16
    for eng in (g.vector, g.scalar):
        eng.wait_ge(T.sem.la, la_total)
        eng.wait_ge(T.sem.xf, xf)
    g.scalar.wait_ge(T.sem.ss, zs)

    for sweep in (1, 2, 3):
        win, own, out = W[(sweep - 1) % 2], R[sweep - 1], R[sweep]
        nwin = W[sweep % 2]
        units = list(range(N)) if sweep < 3 else [(q + 1 + s) % N for s in range(N)]
        pieces = [(p, h) for p in units for h in range(2)]
        if sweep > 1:
            for eng in (g.vector, g.scalar):
                eng.wait_ge(T.sem["fl%d" % (sweep - 1)], 24 * 16)
        g.vector.wait_ge(T.sem.sv, nv[0])

        def offs_of(t):
            p, h = pieces[t]
            c = 128 * p + 64 * h
            return win[:, 0:NV].indirect(T.offs[:, c:c + 64])

        s_done, v_done, scan_done, max_done = {}, {}, {}, {}
        for t in range(10):
            if t not in VSET:
                s_done[t] = sc(g.scalar.activation(T.gat[:, PE * t:PE * t + PE], offs_of(t), ActivationFunctionType.Copy))

        def gather(t):
            v_done[t] = v(g.vector.tensor_copy(T.gat[:, PE * t:PE * t + PE], offs_of(t)))

        def scan(t):
            if t in VSET:
                g.vector.wait_ge(T.sem.sv, v_done[t])
            else:
                g.vector.wait_ge(T.sem.ss, s_done[t])
            scan_done[t] = v(g.vector.tensor_tensor_scan(T.sx[:, PE * t:PE * t + PE], T.pat[:], T.gat[:, PE * t:PE * t + PE],
                                                         0.0, AluOpType.min, AluOpType.max))

        def maxi(t):
            p, h = pieces[t]
            c = 512 * p + HB * h
            g.vector.wait_ge(T.sem.sv, scan_done[t])
            max_done[t] = v(g.vector.tensor_tensor(out[:, c:c + HB], T.sx[:, PE * t + K - 1:PE * t + PE:K], own[:, c:c + HB],
                                                   AluOpType.max))

        gather(VSET[0])
        for t in range(10):
            scan(t)
            if t > 0:
                maxi(t - 1)
            if t == 2:
                gather(VSET[1])
        maxi(9)

        last = N - 1
        if sweep < 3:
            d = [None, T.d1, T.d2][sweep]
            fl = T.sem["fl%d" % sweep]
            for ci, (u0, u1) in enumerate(((0, 2), (2, 4), (4, 5))):
                rd = T.sem["rd%d_%d" % (sweep, ci)]
                tail = u1 == N
                engs = (g.sync, g.scalar) if tail else (g.sync,)
                for u in range(u0, u1):
                    for e, eng in enumerate(engs):
                        eng.wait_ge(T.sem.sv, max_done[2 * u + 1])
                        for r in range(e, 4, len(engs)):
                            eng.dma_start(d[r:r + 1, V * u:V * u + V], out[r:128:16, 512 * u:512 * u + 512]).then_inc(rd, 16)
                for e, eng in enumerate(engs):
                    eng.wait_ge(rd, 64 * (u1 - u0))
                    for gg in range(e, 8, len(engs)):
                        eng.dma_start(nwin[16 * gg:16 * gg + 4, V * u0:V * u1], d[:, V * u0:V * u1]).then_inc(fl, 16)
        else:
            for s, p in enumerate(units):
                rs = T.sem["rs%d" % s]
                engs = (g.sync, g.scalar) if s == last else (g.sync,)
                for e, eng in enumerate(engs):
                    eng.wait_ge(T.sem.sv, max_done[2 * s + 1])
                    for r in range(e, 4, len(engs)):
                        eng.dma_start(T.d3[p, 32 * r:32 * r + 32, :], out[r:128:16, 512 * p:512 * p + 512]).then_inc(rs, 16)
                g.wait_ge(rs, 64)
                a = topo.addr(cores[p])
                m = to_mask(bits(topo.mask(core, cores[p]))[:RET_E])
                g.remote_dma(T.yl[j], T.d3[p], T.sem["ret%d" % s], T.sem.loc, a[1], a[0], m)
                loc += RET_E
    g.wait_ge(T.sem.loc, loc)
